import numpy as np
import ml_dtypes


def mxq(x, axis, fmt="e4m3"):
    dtype, down = {"e4m3": (ml_dtypes.float8_e4m3fn, 7), "e5m2": (ml_dtypes.float8_e5m2, 14)}[fmt]
    v = np.moveaxis(np.asarray(x, np.float32).astype(ml_dtypes.bfloat16).astype(np.float64), axis, -1)
    blocks = v.reshape(v.shape[:-1] + (-1, 32))
    amax = np.abs(blocks).max(-1, keepdims=True)
    byte = np.maximum(np.where(amax > 0, np.frexp(amax)[1] - 1 + 127, 0) - down, 1)
    scale = np.exp2(byte - 127.0)
    codes = (blocks / scale).astype(np.float32).astype(dtype).astype(np.float64)
    return np.moveaxis((codes * scale).reshape(v.shape), -1, axis)


WIDE = False


def mx_kscale(k):
    if not WIDE:
        return np.ones(k)
    levels = np.array([10, -10, 5, -5, 0])
    if k % 512:
        return np.exp2(np.random.permutation(np.resize(levels, k // 32))).repeat(32)
    a = np.empty((k // 512, 16))
    for p in range(k // 512):
        a[p, :8] = np.random.permutation(np.resize(levels, 8))
        for g in range(8):
            far = levels[np.abs(levels - a[p, g]) >= 10]
            a[p, g + 8] = far[np.random.randint(len(far))]
    return np.exp2(a.ravel()).repeat(32)


def f64(x):
    return np.asarray(x).astype(np.float64)


def striped(idx):
    return np.tile(idx.reshape(-1, 16).T, (8, 1)).astype(np.uint16)


def unstriped(offs):
    return offs[:16].T.reshape(-1).astype(np.int64)


E2M1 = np.array([0.0, 0.5, 1.0, 1.5, 2.0, 3.0, 4.0, 6.0, -0.0, -0.5, -1.0, -1.5, -2.0, -3.0, -4.0, -6.0])


def pack_weight(w, fmt):
    k, n = w.shape
    w = f64(np.asarray(w, np.float32).astype(ml_dtypes.bfloat16)).reshape(k // 32, 32, n)
    amax = np.abs(w).max(1)
    if fmt == "e4m3":
        byte = np.frexp(amax)[1] - 1 + 127 - 7
    else:
        mant, ex = np.frexp(amax / 6.0)
        byte = np.where(mant > 0.5, ex, ex - 1) + 127
    byte = np.clip(np.where(amax > 0, byte, 1), 1, 254)
    scaled = (w * np.exp2(127.0 - byte)[:, None, :]).reshape(k, n).astype(np.float32)
    by_word = np.ascontiguousarray(scaled.reshape(k // 512, 128, 4, n).transpose(0, 1, 3, 2))
    if fmt == "e4m3":
        words = by_word.astype(ml_dtypes.float8_e4m3fn).view(np.uint8)
    else:
        c = by_word.astype(ml_dtypes.float4_e2m1fn).view(np.uint8) & 0xF
        words = (c[..., 0::2] | (c[..., 1::2] << 4)).reshape(k // 512, 128, 2 * n)
    return np.ascontiguousarray(words), np.ascontiguousarray(byte.astype(np.uint8).reshape(k // 512, 16, n))


def unpack_weight(words, scales, fmt):
    g, _, n = scales.shape
    words = np.ascontiguousarray(words).reshape(g, 128, n, -1)
    if fmt == "e4m3":
        vals = words.view(ml_dtypes.float8_e4m3fn).astype(np.float64)
    else:
        nib = np.empty((g, 128, n, 4), np.uint8)
        nib[..., 0::2] = words & 0xF
        nib[..., 1::2] = words >> 4
        vals = E2M1[nib]
    vals = vals * np.repeat(np.exp2(scales.astype(np.float64) - 127.0), 8, axis=1)[..., None]
    return vals.transpose(0, 1, 3, 2).reshape(g * 512, n)


def gelu(v):
    return 0.5 * v * (1.0 + np.tanh(np.sqrt(2.0 / np.pi) * (v + 0.044715 * v**3)))


def striped8(idx):
    return np.concatenate([v.reshape(-1, 16).T for v in idx]).astype(np.uint16)


def unstriped8(offs):
    return np.stack([offs[16 * g:16 * g + 16].T.reshape(-1) for g in range(8)]).astype(np.int64)


def put_heads(h, wgs, idx8, t2):
    r = np.arange(h.shape[0])
    page = np.zeros((h.shape[0], t2))
    page[r[:, None], idx8[r % 512 // 64]] = wgs[r // 4 % 128] * h
    return page


K, T, S, T2, P, H, N = 1024, 4096, 1024, 2048, 1024, 512, 512

def setup_inputs():
    n = np.random.standard_normal
    s = mx_kscale(K)[:, None]
    u = mx_kscale(H)[:, None]
    tab_words, tab_scales = pack_weight(n((K, T)) * s, "e4m3")
    w8_words, w8_scales = pack_weight(n((K, N)) / np.sqrt(K) / s, "e4m3")
    w4_words, w4_scales = pack_weight(n((H, N)) / np.sqrt(H) / u, "e2m1")
    slots = np.stack([np.random.permutation(T2)[:S] for _ in range(8)])
    return {
        "tab_words": tab_words, "tab_scales": tab_scales,
        "offs": striped(np.random.permutation(T)[:S]),
        "w1": (1.5 * n((K, H)) / np.sqrt(K) / s).astype(np.float32),
        "gain": (np.exp(0.3 * n(H)) * u[:, 0]).astype(np.float32),
        "wgs": np.repeat(np.random.uniform(0.5, 2.0, (8, S)), 16, axis=0).astype(np.float32),
        "offs2": striped8(slots),
        "offs3": striped(np.random.permutation(T2)[:P]),
        "chan": ((1.2 * n((H, P)) + 0.6) * u).astype(np.float32),
        "lift": (0.5 * n(H) * u[:, 0]).astype(np.float32),
        "w4_words": w4_words, "w4_scales": w4_scales,
        "w2": (0.62 * n((H, N)) / np.sqrt(H) / u).astype(np.float32),
        "w8_words": w8_words, "w8_scales": w8_scales,
    }

def reference(tab_words, tab_scales, offs, w1, gain, wgs, offs2, offs3, chan, lift,
              w4_words, w4_scales, w2, w8_words, w8_scales):
    v = unpack_weight(tab_words, tab_scales, "e4m3")[:, unstriped(offs)]
    pre = mxq(f64(w1), 0, "e4m3").T @ v
    h = f64(gain)[:, None] * (pre / (1.0 + np.exp(-pre)))
    page = put_heads(h, f64(wgs), unstriped8(offs2), T2)
    x = page[:, unstriped(offs3)]
    zq = mxq(np.minimum(x, f64(chan)) + f64(lift)[:, None], 0, "e4m3")
    y1 = unpack_weight(w4_words, w4_scales, "e2m1").T @ zq
    y2 = mxq(f64(w2), 0, "e4m3").T @ zq
    skip = unpack_weight(w8_words, w8_scales, "e4m3").T @ v
    return y1 + np.cos(y2) * skip

@@ -1,0 +1,265 @@
+import math
+from contextlib import ExitStack
+
+import concourse.mybir as mybir
+
+K, T, S, T2, H, N = 1024, 4096, 1024, 2048, 512, 512
+FLOPS = 2 * S * (K * H + K * N + 2 * H * N)
+
+F32 = mybir.dt.float32
+BF16 = mybir.dt.bfloat16
+I32 = mybir.dt.int32
+U32 = mybir.dt.uint32
+U16 = mybir.dt.uint16
+U8 = mybir.dt.uint8
+FP8X4 = mybir.dt.float8_e4m3fn_x4
+FP4X4 = mybir.dt.float4_e2m1fn_x4
+ALU = mybir.AluOpType
+ACT = mybir.ActivationFunctionType
+
+P = 128
+PACK = 4
+PASSES = K // (P * PACK)
+HALF = 512
+CHUNK = 256
+CHUNKS = S // CHUNK
+PAIRS = 2
+ROUND = 1.5 * 2.0**23
+
+
+def tile_list_hydrophone_tap_features_kernel(
+    tc, tab_words, tab_scales, offs, w1, gain, wgs, offs2, offs3, chan, lift,
+    w4_words, w4_scales, w2, w8_words, w8_scales, out,
+):
+    nc = tc.nc
+    with ExitStack() as ctx:
+        keep = ctx.enter_context(tc.tile_pool(name="keep", bufs=1))
+        stage = ctx.enter_context(tc.tile_pool(name="stage", bufs=2))
+        short_banks = ctx.enter_context(tc.psum_pool(name="short_banks", bufs=2))
+        long_banks = ctx.enter_context(tc.psum_pool(name="long_banks", bufs=6))
+
+        def held(shape, dtype, name, tag=None):
+            return keep.tile(shape, dtype, name=name, tag=tag or name, align_bytes=64)
+
+        def entries(lst, first, count):
+            return lst[:, first // 16 : (first + count) // 16]
+
+        list1 = held([P, S // 16], U16, "list1")
+        list2 = held([P, S // 16], U16, "list2")
+        list3 = held([P, S // 16], U16, "list3")
+
+        tab_planes = held([P, T // 4], I32, "tab_planes", tag="planes_then_words")
+        nc.gpsimd.memset(tab_planes[:], 0)
+        for q in range(4):
+            nc.gpsimd.dma_start(
+                tab_planes[32 * q : 32 * q + 8, :], tab_scales[:, 4 * q : 4 * q + 4, :].bitcast(I32)
+            )
+        w_planes = held([P, 2 * N // 4], I32, "w_planes")
+        nc.vector.memset(w_planes[:], 0)
+        pages = [held([P, T2], F32, "page%d" % t) for t in range(PACK)]
+        for t in range(PACK):
+            nc.vector.memset(pages[t][:], 0.0)
+
+        nc.sync.dma_start(list1[:], offs)
+        w1_raw = []
+        for a in range(PASSES):
+            raw = stage.tile([P, PACK, H], F32, name="w1_raw%d" % a, tag="raw")
+            nc.sync.dma_start(
+                raw[:], w1[a * 512 : (a + 1) * 512, :].rearrange("(p j) c -> p j c", j=PACK)
+            )
+            w1_raw.append(raw)
+        tab = [held([P, T], I32, "tab%d" % a) for a in range(PASSES)]
+        gain_sb = held([P, PACK], F32, "gain_sb")
+        lift_sb = held([P, PACK], F32, "lift_sb")
+        wgs_sb = [held([P, HALF], F32, "wgs%d" % s) for s in range(2)]
+        nc.sync.dma_start(tab[0][:], tab_words[0].rearrange("p t i -> p (t i)").bitcast(I32))
+        nc.sync.dma_start(gain_sb[:], gain.rearrange("(p t) -> p t", t=PACK))
+        nc.sync.dma_start(list2[:], offs2)
+        nc.sync.dma_start(tab[1][:], tab_words[1].rearrange("p t i -> p (t i)").bitcast(I32))
+        for s in range(2):
+            nc.sync.dma_start(wgs_sb[s][:], wgs[:, s * HALF : (s + 1) * HALF])
+        nc.sync.dma_start(list3[:], offs3)
+        nc.sync.dma_start(lift_sb[:], lift.rearrange("(p t) -> p t", t=PACK))
+        chan_rows = chan.rearrange("(p t) j -> p t j", t=PACK)
+        ceil = [held([P, S], F32, "ceil%d" % t) for t in range(PACK)]
+        for t in range(PACK):
+            nc.sync.dma_start(ceil[t][:], chan_rows[:, t, :])
+        w8_sb = held([P, PASSES, N], I32, "w8_sb")
+        nc.sync.dma_start(w8_sb[:], w8_words.rearrange("a p c i -> p a (c i)").bitcast(I32))
+        for q in range(4):
+            nc.sync.dma_start(
+                w_planes[32 * q : 32 * q + 8, 0 : N // 4],
+                w8_scales[:, 4 * q : 4 * q + 4, :].bitcast(I32),
+            )
+        w2_raw = stage.tile([P, PACK, N], F32, name="w2_raw", tag="raw")
+        nc.sync.dma_start(w2_raw[:], w2.rearrange("(p j) c -> p j c", j=PACK))
+        w4_sb = held([P, 2 * N // 4], I32, "w4_sb")
+        nc.sync.dma_start(w4_sb[:], w4_words[0].bitcast(I32))
+        for q in range(4):
+            nc.sync.dma_start(
+                w_planes[32 * q : 32 * q + 4, N // 4 : 2 * N // 4],
+                w4_scales[0, 4 * q : 4 * q + 4, :].bitcast(I32),
+            )
+
+        v_scales = held([P, S], U8, "v_scales")
+        nc.vector.tensor_copy(v_scales[:], tab_planes[:].bitcast(U8).indirect(list1[:]))
+        w_scales = w_planes[:].bitcast(U8)
+
+        w1_codes, w1_scales = [], []
+        for a in range(PASSES):
+            grouped = stage.tile([P, H * PACK], BF16, name="w1_grouped%d" % a, tag="grouped", align_bytes=64)
+            nc.scalar.copy(
+                grouped[:].rearrange("p (t m j) -> p m j t", t=PACK, j=PACK),
+                w1_raw[a][:].rearrange("p j (m t) -> p m j t", t=PACK),
+            )
+            codes = held([P, H], U32, "w1_codes%d" % a)
+            scales = held([P, H], U8, "w1_scales%d" % a)
+            nc.vector.quantize_mx(codes[:].bitcast(FP8X4), scales[:], grouped[:])
+            w1_codes.append(codes)
+            w1_scales.append(scales)
+
+        v_words = [held([P, S], U32, "v_words0"), held([P, S], U32, "v_words1", tag="planes_then_words")]
+        for a in range(PASSES):
+            for s in range(2):
+                nc.vector.tensor_copy(
+                    v_words[a][:, s * HALF : (s + 1) * HALF],
+                    tab[a][:].bitcast(U32).indirect(entries(list1, s * HALF, HALF)),
+                )
+
+        def times_v(bank, codes, scales, s):
+            cols = slice(s * HALF, (s + 1) * HALF)
+            for a in range(PASSES):
+                nc.tensor.matmul_mx(
+                    bank[:], lhsT=codes(a), lhsT_scale=scales(a),
+                    rhs=v_words[a][:, cols].bitcast(FP8X4), rhs_scale=v_scales[4 * a : P, cols],
+                    start=(a == 0), stop=(a == PASSES - 1),
+                )
+
+        weight = [held([P, S], F32, "weight%d" % t) for t in range(PACK)]
+
+        def place(t, s):
+            cols = slice(s * HALF, (s + 1) * HALF)
+            rows = slice(t * P, (t + 1) * P)
+            nc.scalar.activation(weight[t][:, cols], wgs_sb[s][:], ACT.Copy, scale=gain_sb[:, t : t + 1])
+            pre = short_banks.tile([P, HALF], F32, name="pre", tag="short")
+            times_v(pre, lambda a: w1_codes[a][:, rows].bitcast(FP8X4), lambda a: w1_scales[a][:, rows], s)
+            last = t == PACK - 1 and s == 1
+            act = held([P, HALF], F32, "act%d_%d" % (t, s), tag="slot1" if last else None)
+            nc.scalar.activation(act[:], pre[:], ACT.Silu)
+            nc.vector.tensor_tensor(
+                pages[t][:].indirect(entries(list2, s * HALF, HALF)), act[:], weight[t][:, cols], ALU.mult
+            )
+
+        def pick(z, c, t):
+            cols = slice(c * CHUNK, (c + 1) * CHUNK)
+            nc.vector.tensor_copy(z[:, t, :], pages[t][:].indirect(entries(list3, c * CHUNK, CHUNK)))
+            nc.vector.scalar_tensor_tensor(
+                z[:, t, :], z[:, t, :], lift_sb[:, t : t + 1], ceil[t][:, cols], ALU.add, ALU.min
+            )
+
+        def z_tile(c):
+            return held([P, PACK, CHUNK], F32, "z%d" % c, tag="slot%d" % (c % 3))
+
+        skip = held([P, N // P, S], F32, "skip")
+
+        def skip_product(nt, s):
+            rows = slice(nt * P, (nt + 1) * P)
+            bank = short_banks.tile([P, HALF], F32, name="skip_bank", tag="short")
+            times_v(bank, lambda a: w8_sb[:, a, rows].bitcast(FP8X4), lambda a: w_scales[4 * a : P, rows], s)
+            nc.scalar.copy(skip[:, nt, s * HALF : (s + 1) * HALF], bank[:])
+
+        z = {0: z_tile(0)}
+        for t in range(PACK):
+            for s in range(2):
+                place(t, s)
+        for t in range(PACK):
+            nc.scalar.activation(ceil[t][:], ceil[t][:], ACT.Identity, bias=lift_sb[:, t : t + 1])
+            pick(z[0], 0, t)
+        for s in range(2):
+            for nt in range(N // P):
+                skip_product(nt, s)
+
+        w2_grouped = stage.tile([P, N * PACK], BF16, name="w2_grouped", tag="grouped", align_bytes=64)
+        nc.scalar.copy(
+            w2_grouped[:].rearrange("p (c i j) -> p c j i", i=4, j=PACK),
+            w2_raw[:].rearrange("p j (c i) -> p c j i", i=4),
+        )
+        w2_codes = held([P, N], U32, "w2_codes")
+        w2_scales = held([P, N], U8, "w2_scales")
+        nc.vector.quantize_mx(w2_codes[:].bitcast(FP8X4), w2_scales[:], w2_grouped[:])
+
+        z_codes, z_scales, turns, spare = {}, {}, {}, {}
+
+        def pick_chunk(c):
+            z[c] = z_tile(c)
+            for t in range(PACK):
+                pick(z[c], c, t)
+
+        grouped_z = {}
+
+        def weave(c):
+            grouped_z[c] = held([P, CHUNK * PACK], BF16, "z_grouped%d" % c, tag="slot%d" % ((c + 2) % 3))
+            nc.scalar.copy(
+                grouped_z[c][:].rearrange("p (c i t) -> p c t i", i=4, t=PACK),
+                z[c][:].rearrange("p t (c i) -> p c t i", i=4),
+            )
+
+        def quantise(c):
+            z_codes[c] = held([P, CHUNK], U32, "z_codes%d" % c)
+            z_scales[c] = held([P, CHUNK], U8, "z_scales%d" % c)
+            nc.vector.quantize_mx(z_codes[c][:].bitcast(FP8X4), z_scales[c][:], grouped_z[c][:])
+
+        def phase(c):
+            for g in range(PAIRS):
+                bank = short_banks.tile([P, 2, CHUNK], F32, name="phase_bank", tag="short")
+                for i in range(2):
+                    rows = slice((2 * g + i) * P, (2 * g + i + 1) * P)
+                    nc.tensor.matmul_mx(
+                        bank[:, i, :], lhsT=w2_codes[:, rows].bitcast(FP8X4), lhsT_scale=w2_scales[:, rows],
+                        rhs=z_codes[c][:].bitcast(FP8X4), rhs_scale=z_scales[c][:], start=True, stop=True,
+                    )
+                turns[c, g] = held([P, 2, CHUNK], F32, "turns%d_%d" % (c, g))
+                spare[c, g] = held([P, 2, CHUNK], F32, "spare%d_%d" % (c, g))
+                nc.scalar.activation(turns[c, g][:], bank[:], ACT.Copy, scale=0.5 / math.pi, bias=0.25)
+                nc.scalar.activation(spare[c, g][:], turns[c, g][:], ACT.Copy, bias=ROUND)
+
+        def reduce_range(c):
+            for g in range(PAIRS):
+                nc.vector.scalar_tensor_tensor(
+                    spare[c, g][:], spare[c, g][:], ROUND, turns[c, g][:], ALU.subtract, ALU.subtract
+                )
+
+        def cosine(c):
+            for g in range(PAIRS):
+                nc.scalar.activation(turns[c, g][:], spare[c, g][:], ACT.Sin, scale=-2.0 * math.pi)
+
+        def finish(c):
+            cols = slice(c * CHUNK, (c + 1) * CHUNK)
+            banks = []
+            for g in range(PAIRS):
+                bank = long_banks.tile([P, 2, CHUNK], F32, name="feature_bank", tag="long")
+                for i in range(2):
+                    nt = 2 * g + i
+                    nc.tensor.matmul_mx(
+                        bank[:, i, :],
+                        lhsT=w4_sb[:].bitcast(U8)[:, nt * 2 * P : (nt + 1) * 2 * P].bitcast(FP4X4),
+                        lhsT_scale=w_scales[:, N + nt * P : N + (nt + 1) * P],
+                        rhs=z_codes[c][:].bitcast(FP8X4), rhs_scale=z_scales[c][:], start=True, stop=True,
+                    )
+                banks.append(bank)
+                nc.vector.tensor_tensor(
+                    spare[c, g][:], turns[c, g][:], skip[:, 2 * g : 2 * g + 2, cols], ALU.mult
+                )
+            for g in range(PAIRS):
+                nc.vector.tensor_tensor(turns[c, g][:], spare[c, g][:], banks[g][:], ALU.add)
+                nc.sync.dma_start(
+                    out[2 * g * P : (2 * g + 2) * P, cols].rearrange("(i p) j -> p i j", p=P), turns[c, g][:]
+                )
+
+        steps = [
+            (1, pick_chunk), (0, weave), (-1, phase), (-2, cosine), (0, quantise), (-1, reduce_range), (-2, finish),
+        ]
+        for step in range(CHUNKS + 2):
+            for shift, work in steps:
+                if 0 <= step + shift < CHUNKS:
+                    work(step + shift)

@@ -50,17 +50,15 @@ def tile_list_hydrophone_tap_features_kernel(
 
         tab_planes = held([P, T // 4], I32, "tab_planes", tag="planes_then_words")
         nc.gpsimd.memset(tab_planes[:], 0)
-        for q in range(4):
-            nc.gpsimd.dma_start(
-                tab_planes[32 * q : 32 * q + 8, :], tab_scales[:, 4 * q : 4 * q + 4, :].bitcast(I32)
-            )
         w_planes = held([P, 2 * N // 4], I32, "w_planes")
-        nc.vector.memset(w_planes[:], 0)
+        nc.gpsimd.memset(w_planes[:], 0)
         pages = [held([P, T2], F32, "page%d" % t) for t in range(PACK)]
         for t in range(PACK):
-            nc.vector.memset(pages[t][:], 0.0)
+            nc.gpsimd.memset(pages[t][:], 0.0)
 
         nc.sync.dma_start(list1[:], offs)
+        tab = [held([P, T], I32, "tab%d" % a) for a in range(PASSES)]
+        nc.sync.dma_start(tab[0][:], tab_words[0].rearrange("p t i -> p (t i)").bitcast(I32))
         w1_raw = []
         for a in range(PASSES):
             raw = stage.tile([P, PACK, H], F32, name="w1_raw%d" % a, tag="raw")
@@ -68,14 +66,18 @@ def tile_list_hydrophone_tap_features_kernel(
                 raw[:], w1[a * 512 : (a + 1) * 512, :].rearrange("(p j) c -> p j c", j=PACK)
             )
             w1_raw.append(raw)
-        tab = [held([P, T], I32, "tab%d" % a) for a in range(PASSES)]
+        for a in range(PASSES):
+            for q in range(4):
+                nc.sync.dma_start(
+                    tab_planes[32 * q + 4 * a : 32 * q + 4 * a + 4, :],
+                    tab_scales[a, 4 * q : 4 * q + 4, :].bitcast(I32),
+                )
         gain_sb = held([P, PACK], F32, "gain_sb")
         lift_sb = held([P, PACK], F32, "lift_sb")
         wgs_sb = [held([P, HALF], F32, "wgs%d" % s) for s in range(2)]
-        nc.sync.dma_start(tab[0][:], tab_words[0].rearrange("p t i -> p (t i)").bitcast(I32))
+        nc.sync.dma_start(tab[1][:], tab_words[1].rearrange("p t i -> p (t i)").bitcast(I32))
         nc.sync.dma_start(gain_sb[:], gain.rearrange("(p t) -> p t", t=PACK))
         nc.sync.dma_start(list2[:], offs2)
-        nc.sync.dma_start(tab[1][:], tab_words[1].rearrange("p t i -> p (t i)").bitcast(I32))
         for s in range(2):
             nc.sync.dma_start(wgs_sb[s][:], wgs[:, s * HALF : (s + 1) * HALF])
         nc.sync.dma_start(list3[:], offs3)
@@ -150,9 +152,11 @@ def tile_list_hydrophone_tap_features_kernel(
                 pages[t][:].indirect(entries(list2, s * HALF, HALF)), act[:], weight[t][:, cols], ALU.mult
             )
 
-        def pick(z, c, t):
-            cols = slice(c * CHUNK, (c + 1) * CHUNK)
+        def fetch(z, c, t):
             nc.vector.tensor_copy(z[:, t, :], pages[t][:].indirect(entries(list3, c * CHUNK, CHUNK)))
+
+        def limit(z, c, t):
+            cols = slice(c * CHUNK, (c + 1) * CHUNK)
             nc.vector.scalar_tensor_tensor(
                 z[:, t, :], z[:, t, :], lift_sb[:, t : t + 1], ceil[t][:, cols], ALU.add, ALU.min
             )
@@ -169,12 +173,14 @@ def tile_list_hydrophone_tap_features_kernel(
             nc.scalar.copy(skip[:, nt, s * HALF : (s + 1) * HALF], bank[:])
 
         z = {0: z_tile(0)}
-        for t in range(PACK):
-            for s in range(2):
+        for s in range(2):
+            for t in range(PACK):
                 place(t, s)
         for t in range(PACK):
             nc.scalar.activation(ceil[t][:], ceil[t][:], ACT.Identity, bias=lift_sb[:, t : t + 1])
-            pick(z[0], 0, t)
+            fetch(z[0], 0, t)
+        for t in range(PACK):
+            limit(z[0], 0, t)
         for s in range(2):
             for nt in range(N // P):
                 skip_product(nt, s)
@@ -193,7 +199,9 @@ def tile_list_hydrophone_tap_features_kernel(
         def pick_chunk(c):
             z[c] = z_tile(c)
             for t in range(PACK):
-                pick(z[c], c, t)
+                fetch(z[c], c, t)
+            for t in range(PACK):
+                limit(z[c], c, t)
 
         grouped_z = {}
 

@@ -2,6 +2,7 @@ import math
 from contextlib import ExitStack
 
 import concourse.mybir as mybir
+from concourse.masks import make_identity
 
 K, T, S, T2, H, N = 1024, 4096, 1024, 2048, 512, 512
 FLOPS = 2 * S * (K * H + K * N + 2 * H * N)
@@ -25,6 +26,7 @@ CHUNK = 256
 CHUNKS = S // CHUNK
 PAIRS = 2
 ROUND = 1.5 * 2.0**23
+ROUNDED_ON_SCALAR = 2
 
 
 def tile_list_hydrophone_tap_features_kernel(
@@ -36,7 +38,9 @@ def tile_list_hydrophone_tap_features_kernel(
         keep = ctx.enter_context(tc.tile_pool(name="keep", bufs=1))
         stage = ctx.enter_context(tc.tile_pool(name="stage", bufs=2))
         short_banks = ctx.enter_context(tc.psum_pool(name="short_banks", bufs=2))
-        long_banks = ctx.enter_context(tc.psum_pool(name="long_banks", bufs=6))
+        wrap_banks = ctx.enter_context(tc.psum_pool(name="wrap_banks", bufs=2))
+        long_banks = ctx.enter_context(tc.psum_pool(name="long_banks", bufs=4))
+        ring = ctx.enter_context(tc.tile_pool(name="ring", bufs=4))
 
         def held(shape, dtype, name, tag=None):
             return keep.tile(shape, dtype, name=name, tag=tag or name, align_bytes=64)
@@ -48,40 +52,51 @@ def tile_list_hydrophone_tap_features_kernel(
         list2 = held([P, S // 16], U16, "list2")
         list3 = held([P, S // 16], U16, "list3")
 
-        tab_planes = held([P, T // 4], I32, "tab_planes", tag="planes_then_words")
+        tab_planes = held([P, T // 4], I32, "tab_planes", tag="codes1")
         nc.gpsimd.memset(tab_planes[:], 0)
         w_planes = held([P, 2 * N // 4], I32, "w_planes")
         nc.gpsimd.memset(w_planes[:], 0)
         pages = [held([P, T2], F32, "page%d" % t) for t in range(PACK)]
         for t in range(PACK):
             nc.gpsimd.memset(pages[t][:], 0.0)
+        identity = held([P, P], F32, "identity")
+        make_identity(nc, identity[:])
+        magic = held([P, P], F32, "magic")
+        nc.gpsimd.memset(magic[:], ROUND)
 
+        gain_sb = held([P, PACK], F32, "gain_sb")
+        lift_sb = held([P, PACK], F32, "lift_sb")
         nc.sync.dma_start(list1[:], offs)
         tab = [held([P, T], I32, "tab%d" % a) for a in range(PASSES)]
-        nc.sync.dma_start(tab[0][:], tab_words[0].rearrange("p t i -> p (t i)").bitcast(I32))
-        w1_raw = []
-        for a in range(PASSES):
-            raw = stage.tile([P, PACK, H], F32, name="w1_raw%d" % a, tag="raw")
-            nc.sync.dma_start(
-                raw[:], w1[a * 512 : (a + 1) * 512, :].rearrange("(p j) c -> p j c", j=PACK)
-            )
-            w1_raw.append(raw)
-        for a in range(PASSES):
+        tab_rows = tab_words.rearrange("a p t i -> a p (t i)").bitcast(I32)
+        for first in (0, T // 2):
+            nc.sync.dma_start(tab[0][:, first : first + T // 2], tab_rows[0, :, first : first + T // 2])
+        nc.sync.dma_start(list2[:], offs2)
+        nc.sync.dma_start(list3[:], offs3)
+        nc.sync.dma_start(gain_sb[:], gain.rearrange("(p t) -> p t", t=PACK))
+        nc.sync.dma_start(lift_sb[:], lift.rearrange("(p t) -> p t", t=PACK))
+
+        def load_tab_scales(a):
             for q in range(4):
                 nc.sync.dma_start(
                     tab_planes[32 * q + 4 * a : 32 * q + 4 * a + 4, :],
                     tab_scales[a, 4 * q : 4 * q + 4, :].bitcast(I32),
                 )
-        gain_sb = held([P, PACK], F32, "gain_sb")
-        lift_sb = held([P, PACK], F32, "lift_sb")
+
+        w1_raw = []
+        for a in range(PASSES):
+            if a == 1:
+                load_tab_scales(0)
+            raw = stage.tile([P, PACK, H], F32, name="w1_raw%d" % a, tag="raw")
+            nc.sync.dma_start(
+                raw[:], w1[a * 512 : (a + 1) * 512, :].rearrange("(p j) c -> p j c", j=PACK)
+            )
+            w1_raw.append(raw)
+        load_tab_scales(1)
         wgs_sb = [held([P, HALF], F32, "wgs%d" % s) for s in range(2)]
-        nc.sync.dma_start(tab[1][:], tab_words[1].rearrange("p t i -> p (t i)").bitcast(I32))
-        nc.sync.dma_start(gain_sb[:], gain.rearrange("(p t) -> p t", t=PACK))
-        nc.sync.dma_start(list2[:], offs2)
+        nc.sync.dma_start(tab[1][:], tab_rows[1])
         for s in range(2):
             nc.sync.dma_start(wgs_sb[s][:], wgs[:, s * HALF : (s + 1) * HALF])
-        nc.sync.dma_start(list3[:], offs3)
-        nc.sync.dma_start(lift_sb[:], lift.rearrange("(p t) -> p t", t=PACK))
         chan_rows = chan.rearrange("(p t) j -> p t j", t=PACK)
         ceil = [held([P, S], F32, "ceil%d" % t) for t in range(PACK)]
         for t in range(PACK):
@@ -109,18 +124,18 @@ def tile_list_hydrophone_tap_features_kernel(
 
         w1_codes, w1_scales = [], []
         for a in range(PASSES):
-            grouped = stage.tile([P, H * PACK], BF16, name="w1_grouped%d" % a, tag="grouped", align_bytes=64)
+            grouped = held([P, H * PACK], BF16, "w1_grouped%d" % a, tag="grouped%d" % a)
             nc.scalar.copy(
                 grouped[:].rearrange("p (t m j) -> p m j t", t=PACK, j=PACK),
                 w1_raw[a][:].rearrange("p j (m t) -> p m j t", t=PACK),
             )
-            codes = held([P, H], U32, "w1_codes%d" % a)
+            codes = held([P, H], U32, "w1_codes%d" % a, tag="codes%d" % a)
             scales = held([P, H], U8, "w1_scales%d" % a)
             nc.vector.quantize_mx(codes[:].bitcast(FP8X4), scales[:], grouped[:])
             w1_codes.append(codes)
             w1_scales.append(scales)
 
-        v_words = [held([P, S], U32, "v_words0"), held([P, S], U32, "v_words1", tag="planes_then_words")]
+        v_words = [held([P, S], U32, "v_words0"), held([P, S], U32, "v_words1", tag="grouped1")]
         for a in range(PASSES):
             for s in range(2):
                 nc.vector.tensor_copy(
@@ -128,28 +143,29 @@ def tile_list_hydrophone_tap_features_kernel(
                     tab[a][:].bitcast(U32).indirect(entries(list1, s * HALF, HALF)),
                 )
 
-        def times_v(bank, codes, scales, s):
-            cols = slice(s * HALF, (s + 1) * HALF)
+        def times_v(bank, codes, scales, cols):
             for a in range(PASSES):
                 nc.tensor.matmul_mx(
-                    bank[:], lhsT=codes(a), lhsT_scale=scales(a),
+                    bank, lhsT=codes(a), lhsT_scale=scales(a),
                     rhs=v_words[a][:, cols].bitcast(FP8X4), rhs_scale=v_scales[4 * a : P, cols],
                     start=(a == 0), stop=(a == PASSES - 1),
                 )
 
-        weight = [held([P, S], F32, "weight%d" % t) for t in range(PACK)]
-
-        def place(t, s):
-            cols = slice(s * HALF, (s + 1) * HALF)
+        def place(t, first, count):
             rows = slice(t * P, (t + 1) * P)
-            nc.scalar.activation(weight[t][:, cols], wgs_sb[s][:], ACT.Copy, scale=gain_sb[:, t : t + 1])
-            pre = short_banks.tile([P, HALF], F32, name="pre", tag="short")
-            times_v(pre, lambda a: w1_codes[a][:, rows].bitcast(FP8X4), lambda a: w1_scales[a][:, rows], s)
-            last = t == PACK - 1 and s == 1
-            act = held([P, HALF], F32, "act%d_%d" % (t, s), tag="slot1" if last else None)
+            pre = short_banks.tile([P, count], F32, name="pre", tag="short")
+            times_v(
+                pre[:], lambda a: w1_codes[a][:, rows].bitcast(FP8X4), lambda a: w1_scales[a][:, rows],
+                slice(first, first + count),
+            )
+            last = t == PACK - 1 and first + count == S
+            act = held([P, count], F32, "act%d_%d" % (t, first), tag="slot1" if last else None)
             nc.scalar.activation(act[:], pre[:], ACT.Silu)
+            nc.scalar.activation(act[:], act[:], ACT.Copy, scale=gain_sb[:, t : t + 1])
+            within = first % HALF
             nc.vector.tensor_tensor(
-                pages[t][:].indirect(entries(list2, s * HALF, HALF)), act[:], weight[t][:, cols], ALU.mult
+                pages[t][:].indirect(entries(list2, first, count)), act[:],
+                wgs_sb[first // HALF][:, within : within + count], ALU.mult,
             )
 
         def fetch(z, c, t):
@@ -169,13 +185,18 @@ def tile_list_hydrophone_tap_features_kernel(
         def skip_product(nt, s):
             rows = slice(nt * P, (nt + 1) * P)
             bank = short_banks.tile([P, HALF], F32, name="skip_bank", tag="short")
-            times_v(bank, lambda a: w8_sb[:, a, rows].bitcast(FP8X4), lambda a: w_scales[4 * a : P, rows], s)
+            times_v(
+                bank[:], lambda a: w8_sb[:, a, rows].bitcast(FP8X4), lambda a: w_scales[4 * a : P, rows],
+                slice(s * HALF, (s + 1) * HALF),
+            )
             nc.scalar.copy(skip[:, nt, s * HALF : (s + 1) * HALF], bank[:])
 
         z = {0: z_tile(0)}
-        for s in range(2):
-            for t in range(PACK):
-                place(t, s)
+        quarter = HALF // 2
+        for t, first, count in [(0, 0, quarter), (1, 0, HALF), (0, quarter, quarter), (2, 0, HALF), (3, 0, HALF)]:
+            place(t, first, count)
+        for t in range(PACK):
+            place(t, HALF, HALF)
         for t in range(PACK):
             nc.scalar.activation(ceil[t][:], ceil[t][:], ACT.Identity, bias=lift_sb[:, t : t + 1])
             fetch(z[0], 0, t)
@@ -185,7 +206,7 @@ def tile_list_hydrophone_tap_features_kernel(
             for nt in range(N // P):
                 skip_product(nt, s)
 
-        w2_grouped = stage.tile([P, N * PACK], BF16, name="w2_grouped", tag="grouped", align_bytes=64)
+        w2_grouped = held([P, N * PACK], BF16, "w2_grouped", tag="grouped0")
         nc.scalar.copy(
             w2_grouped[:].rearrange("p (c i j) -> p c j i", i=4, j=PACK),
             w2_raw[:].rearrange("p j (c i) -> p c j i", i=4),
@@ -194,7 +215,7 @@ def tile_list_hydrophone_tap_features_kernel(
         w2_scales = held([P, N], U8, "w2_scales")
         nc.vector.quantize_mx(w2_codes[:].bitcast(FP8X4), w2_scales[:], w2_grouped[:])
 
-        z_codes, z_scales, turns, spare = {}, {}, {}, {}
+        z_codes, z_scales, turns, whole, result = {}, {}, {}, {}, {}
 
         def pick_chunk(c):
             z[c] = z_tile(c)
@@ -218,28 +239,38 @@ def tile_list_hydrophone_tap_features_kernel(
             nc.vector.quantize_mx(z_codes[c][:].bitcast(FP8X4), z_scales[c][:], grouped_z[c][:])
 
         def phase(c):
-            for g in range(PAIRS):
-                bank = short_banks.tile([P, 2, CHUNK], F32, name="phase_bank", tag="short")
-                for i in range(2):
-                    rows = slice((2 * g + i) * P, (2 * g + i + 1) * P)
-                    nc.tensor.matmul_mx(
-                        bank[:, i, :], lhsT=w2_codes[:, rows].bitcast(FP8X4), lhsT_scale=w2_scales[:, rows],
-                        rhs=z_codes[c][:].bitcast(FP8X4), rhs_scale=z_scales[c][:], start=True, stop=True,
-                    )
-                turns[c, g] = held([P, 2, CHUNK], F32, "turns%d_%d" % (c, g))
-                spare[c, g] = held([P, 2, CHUNK], F32, "spare%d_%d" % (c, g))
-                nc.scalar.activation(turns[c, g][:], bank[:], ACT.Copy, scale=0.5 / math.pi, bias=0.25)
-                nc.scalar.activation(spare[c, g][:], turns[c, g][:], ACT.Copy, bias=ROUND)
-
-        def reduce_range(c):
-            for g in range(PAIRS):
-                nc.vector.scalar_tensor_tensor(
-                    spare[c, g][:], spare[c, g][:], ROUND, turns[c, g][:], ALU.subtract, ALU.subtract
+            for h in range(CHUNK // P):
+                taps = slice(h * P, (h + 1) * P)
+                bank = short_banks.tile([P, N], F32, name="phase_bank", tag="short")
+                nc.tensor.matmul_mx(
+                    bank[:], lhsT=z_codes[c][:, taps].bitcast(FP8X4), lhsT_scale=z_scales[c][:, taps],
+                    rhs=w2_codes[:].bitcast(FP8X4), rhs_scale=w2_scales[:], start=True, stop=True,
                 )
+                turns[c, h] = ring.tile([P, N], F32, name="turns")
+                whole[c, h] = ring.tile([P, N], F32, name="whole")
+                nc.scalar.activation(turns[c, h][:], bank[:], ACT.Copy, scale=0.5 / math.pi, bias=0.25)
+                if c < ROUNDED_ON_SCALAR:
+                    nc.scalar.activation(whole[c, h][:], turns[c, h][:], ACT.Copy, scale=-1.0, bias=-ROUND)
+
+        def round_turns(c):
+            if c >= ROUNDED_ON_SCALAR:
+                for h in range(CHUNK // P):
+                    nc.vector.tensor_scalar(whole[c, h][:], turns[c, h][:], -1.0, -ROUND, ALU.mult, ALU.add)
 
         def cosine(c):
             for g in range(PAIRS):
-                nc.scalar.activation(turns[c, g][:], spare[c, g][:], ACT.Sin, scale=-2.0 * math.pi)
+                bank = wrap_banks.tile([P, 2, CHUNK], F32, name="wrap_bank")
+                for h in range(CHUNK // P):
+                    for i in range(2):
+                        rows = slice((2 * g + i) * P, (2 * g + i + 1) * P)
+                        terms = (magic[:], whole[c, h][:, rows], turns[c, h][:, rows])
+                        for n, term in enumerate(terms):
+                            nc.tensor.matmul(
+                                bank[:, i, h * P : (h + 1) * P], lhsT=term, rhs=identity[:],
+                                is_transpose=True, start=(n == 0), stop=(n == len(terms) - 1),
+                            )
+                result[c, g] = held([P, 2, CHUNK], F32, "result%d_%d" % (c, g))
+                nc.scalar.activation(result[c, g][:], bank[:], ACT.Sin, scale=2.0 * math.pi)
 
         def finish(c):
             cols = slice(c * CHUNK, (c + 1) * CHUNK)
@@ -256,16 +287,16 @@ def tile_list_hydrophone_tap_features_kernel(
                     )
                 banks.append(bank)
                 nc.vector.tensor_tensor(
-                    spare[c, g][:], turns[c, g][:], skip[:, 2 * g : 2 * g + 2, cols], ALU.mult
+                    result[c, g][:], result[c, g][:], skip[:, 2 * g : 2 * g + 2, cols], ALU.mult
                 )
             for g in range(PAIRS):
-                nc.vector.tensor_tensor(turns[c, g][:], spare[c, g][:], banks[g][:], ALU.add)
+                nc.vector.tensor_tensor(result[c, g][:], result[c, g][:], banks[g][:], ALU.add)
                 nc.sync.dma_start(
-                    out[2 * g * P : (2 * g + 2) * P, cols].rearrange("(i p) j -> p i j", p=P), turns[c, g][:]
+                    out[2 * g * P : (2 * g + 2) * P, cols].rearrange("(i p) j -> p i j", p=P), result[c, g][:]
                 )
 
         steps = [
-            (1, pick_chunk), (0, weave), (-1, phase), (-2, cosine), (0, quantise), (-1, reduce_range), (-2, finish),
+            (1, pick_chunk), (0, weave), (-1, phase), (-2, cosine), (0, quantise), (-1, round_turns), (-2, finish),
         ]
         for step in range(CHUNKS + 2):
             for shift, work in steps:

import math
from contextlib import ExitStack

import concourse.mybir as mybir
from concourse.masks import make_identity

K, T, S, T2, H, N = 1024, 4096, 1024, 2048, 512, 512
FLOPS = 2 * S * (K * H + K * N + 2 * H * N)

F32 = mybir.dt.float32
BF16 = mybir.dt.bfloat16
I32 = mybir.dt.int32
U32 = mybir.dt.uint32
U16 = mybir.dt.uint16
U8 = mybir.dt.uint8
FP8X4 = mybir.dt.float8_e4m3fn_x4
FP4X4 = mybir.dt.float4_e2m1fn_x4
ALU = mybir.AluOpType
ACT = mybir.ActivationFunctionType

P = 128
PACK = 4
PASSES = K // (P * PACK)
HALF = 512
CHUNK = 256
CHUNKS = S // CHUNK
PAIRS = 2
ROUND = 1.5 * 2.0**23
ROUNDED_ON_SCALAR = 2


def tile_list_hydrophone_tap_features_kernel(
    tc, tab_words, tab_scales, offs, w1, gain, wgs, offs2, offs3, chan, lift,
    w4_words, w4_scales, w2, w8_words, w8_scales, out,
):
    nc = tc.nc
    with ExitStack() as ctx:
        keep = ctx.enter_context(tc.tile_pool(name="keep", bufs=1))
        stage = ctx.enter_context(tc.tile_pool(name="stage", bufs=2))
        short_banks = ctx.enter_context(tc.psum_pool(name="short_banks", bufs=2))
        wrap_banks = ctx.enter_context(tc.psum_pool(name="wrap_banks", bufs=2))
        long_banks = ctx.enter_context(tc.psum_pool(name="long_banks", bufs=4))
        ring = ctx.enter_context(tc.tile_pool(name="ring", bufs=4))

        def held(shape, dtype, name, tag=None):
            return keep.tile(shape, dtype, name=name, tag=tag or name, align_bytes=64)

        def entries(lst, first, count):
            return lst[:, first // 16 : (first + count) // 16]

        list1 = held([P, S // 16], U16, "list1")
        list2 = held([P, S // 16], U16, "list2")
        list3 = held([P, S // 16], U16, "list3")

        tab_planes = held([P, T // 4], I32, "tab_planes", tag="codes1")
        nc.gpsimd.memset(tab_planes[:], 0)
        w_planes = held([P, 2 * N // 4], I32, "w_planes")
        nc.gpsimd.memset(w_planes[:], 0)
        pages = [held([P, T2], F32, "page%d" % t) for t in range(PACK)]
        for t in range(PACK):
            nc.gpsimd.memset(pages[t][:], 0.0)
        identity = held([P, P], F32, "identity")
        make_identity(nc, identity[:])
        magic = held([P, P], F32, "magic")
        nc.gpsimd.memset(magic[:], ROUND)

        gain_sb = held([P, PACK], F32, "gain_sb")
        lift_sb = held([P, PACK], F32, "lift_sb")
        nc.sync.dma_start(list1[:], offs)
        tab = [held([P, T], I32, "tab%d" % a) for a in range(PASSES)]
        tab_rows = tab_words.rearrange("a p t i -> a p (t i)").bitcast(I32)
        for first in (0, T // 2):
            nc.sync.dma_start(tab[0][:, first : first + T // 2], tab_rows[0, :, first : first + T // 2])
        nc.sync.dma_start(list2[:], offs2)
        nc.sync.dma_start(list3[:], offs3)
        nc.sync.dma_start(gain_sb[:], gain.rearrange("(p t) -> p t", t=PACK))
        nc.sync.dma_start(lift_sb[:], lift.rearrange("(p t) -> p t", t=PACK))

        def load_tab_scales(a):
            for q in range(4):
                nc.sync.dma_start(
                    tab_planes[32 * q + 4 * a : 32 * q + 4 * a + 4, :],
                    tab_scales[a, 4 * q : 4 * q + 4, :].bitcast(I32),
                )

        w1_raw = []
        for a in range(PASSES):
            if a == 1:
                load_tab_scales(0)
            raw = stage.tile([P, PACK, H], F32, name="w1_raw%d" % a, tag="raw")
            nc.sync.dma_start(
                raw[:], w1[a * 512 : (a + 1) * 512, :].rearrange("(p j) c -> p j c", j=PACK)
            )
            w1_raw.append(raw)
        load_tab_scales(1)
        wgs_sb = [held([P, HALF], F32, "wgs%d" % s) for s in range(2)]
        nc.sync.dma_start(tab[1][:], tab_rows[1])
        for s in range(2):
            nc.sync.dma_start(wgs_sb[s][:], wgs[:, s * HALF : (s + 1) * HALF])
        chan_rows = chan.rearrange("(p t) j -> p t j", t=PACK)
        ceil = [held([P, S], F32, "ceil%d" % t) for t in range(PACK)]
        for t in range(PACK):
            nc.sync.dma_start(ceil[t][:], chan_rows[:, t, :])
        w8_sb = held([P, PASSES, N], I32, "w8_sb")
        nc.sync.dma_start(w8_sb[:], w8_words.rearrange("a p c i -> p a (c i)").bitcast(I32))
        for q in range(4):
            nc.sync.dma_start(
                w_planes[32 * q : 32 * q + 8, 0 : N // 4],
                w8_scales[:, 4 * q : 4 * q + 4, :].bitcast(I32),
            )
        w2_raw = stage.tile([P, PACK, N], F32, name="w2_raw", tag="raw")
        nc.sync.dma_start(w2_raw[:], w2.rearrange("(p j) c -> p j c", j=PACK))
        w4_sb = held([P, 2 * N // 4], I32, "w4_sb")
        nc.sync.dma_start(w4_sb[:], w4_words[0].bitcast(I32))
        for q in range(4):
            nc.sync.dma_start(
                w_planes[32 * q : 32 * q + 4, N // 4 : 2 * N // 4],
                w4_scales[0, 4 * q : 4 * q + 4, :].bitcast(I32),
            )

        v_scales = held([P, S], U8, "v_scales")
        nc.vector.tensor_copy(v_scales[:], tab_planes[:].bitcast(U8).indirect(list1[:]))
        w_scales = w_planes[:].bitcast(U8)

        w1_codes, w1_scales = [], []
        for a in range(PASSES):
            grouped = held([P, H * PACK], BF16, "w1_grouped%d" % a, tag="grouped%d" % a)
            nc.scalar.copy(
                grouped[:].rearrange("p (t m j) -> p m j t", t=PACK, j=PACK),
                w1_raw[a][:].rearrange("p j (m t) -> p m j t", t=PACK),
            )
            codes = held([P, H], U32, "w1_codes%d" % a, tag="codes%d" % a)
            scales = held([P, H], U8, "w1_scales%d" % a)
            nc.vector.quantize_mx(codes[:].bitcast(FP8X4), scales[:], grouped[:])
            w1_codes.append(codes)
            w1_scales.append(scales)

        v_words = [held([P, S], U32, "v_words0"), held([P, S], U32, "v_words1", tag="grouped1")]
        for a in range(PASSES):
            for s in range(2):
                nc.vector.tensor_copy(
                    v_words[a][:, s * HALF : (s + 1) * HALF],
                    tab[a][:].bitcast(U32).indirect(entries(list1, s * HALF, HALF)),
                )

        def times_v(bank, codes, scales, cols):
            for a in range(PASSES):
                nc.tensor.matmul_mx(
                    bank, lhsT=codes(a), lhsT_scale=scales(a),
                    rhs=v_words[a][:, cols].bitcast(FP8X4), rhs_scale=v_scales[4 * a : P, cols],
                    start=(a == 0), stop=(a == PASSES - 1),
                )

        def place(t, first, count):
            rows = slice(t * P, (t + 1) * P)
            pre = short_banks.tile([P, count], F32, name="pre", tag="short")
            times_v(
                pre[:], lambda a: w1_codes[a][:, rows].bitcast(FP8X4), lambda a: w1_scales[a][:, rows],
                slice(first, first + count),
            )
            last = t == PACK - 1 and first + count == S
            act = held([P, count], F32, "act%d_%d" % (t, first), tag="slot1" if last else None)
            nc.scalar.activation(act[:], pre[:], ACT.Silu)
            nc.scalar.activation(act[:], act[:], ACT.Copy, scale=gain_sb[:, t : t + 1])
            within = first % HALF
            nc.vector.tensor_tensor(
                pages[t][:].indirect(entries(list2, first, count)), act[:],
                wgs_sb[first // HALF][:, within : within + count], ALU.mult,
            )

        def fetch(z, c, t):
            nc.vector.tensor_copy(z[:, t, :], pages[t][:].indirect(entries(list3, c * CHUNK, CHUNK)))

        def limit(z, c, t):
            cols = slice(c * CHUNK, (c + 1) * CHUNK)
            nc.vector.scalar_tensor_tensor(
                z[:, t, :], z[:, t, :], lift_sb[:, t : t + 1], ceil[t][:, cols], ALU.add, ALU.min
            )

        def z_tile(c):
            return held([P, PACK, CHUNK], F32, "z%d" % c, tag="slot%d" % (c % 3))

        skip = held([P, N // P, S], F32, "skip")

        def skip_product(nt, s):
            rows = slice(nt * P, (nt + 1) * P)
            bank = short_banks.tile([P, HALF], F32, name="skip_bank", tag="short")
            times_v(
                bank[:], lambda a: w8_sb[:, a, rows].bitcast(FP8X4), lambda a: w_scales[4 * a : P, rows],
                slice(s * HALF, (s + 1) * HALF),
            )
            nc.scalar.copy(skip[:, nt, s * HALF : (s + 1) * HALF], bank[:])

        z = {0: z_tile(0)}
        quarter = HALF // 2
        for t, first, count in [(0, 0, quarter), (1, 0, HALF), (0, quarter, quarter), (2, 0, HALF), (3, 0, HALF)]:
            place(t, first, count)
        for t in range(PACK):
            place(t, HALF, HALF)
        for t in range(PACK):
            nc.scalar.activation(ceil[t][:], ceil[t][:], ACT.Identity, bias=lift_sb[:, t : t + 1])
            fetch(z[0], 0, t)
        for t in range(PACK):
            limit(z[0], 0, t)
        for s in range(2):
            for nt in range(N // P):
                skip_product(nt, s)

        w2_grouped = held([P, N * PACK], BF16, "w2_grouped", tag="grouped0")
        nc.scalar.copy(
            w2_grouped[:].rearrange("p (c i j) -> p c j i", i=4, j=PACK),
            w2_raw[:].rearrange("p j (c i) -> p c j i", i=4),
        )
        w2_codes = held([P, N], U32, "w2_codes")
        w2_scales = held([P, N], U8, "w2_scales")
        nc.vector.quantize_mx(w2_codes[:].bitcast(FP8X4), w2_scales[:], w2_grouped[:])

        z_codes, z_scales, turns, whole, result = {}, {}, {}, {}, {}

        def pick_chunk(c):
            z[c] = z_tile(c)
            for t in range(PACK):
                fetch(z[c], c, t)
            for t in range(PACK):
                limit(z[c], c, t)

        grouped_z = {}

        def weave(c):
            grouped_z[c] = held([P, CHUNK * PACK], BF16, "z_grouped%d" % c, tag="slot%d" % ((c + 2) % 3))
            nc.scalar.copy(
                grouped_z[c][:].rearrange("p (c i t) -> p c t i", i=4, t=PACK),
                z[c][:].rearrange("p t (c i) -> p c t i", i=4),
            )

        def quantise(c):
            z_codes[c] = held([P, CHUNK], U32, "z_codes%d" % c)
            z_scales[c] = held([P, CHUNK], U8, "z_scales%d" % c)
            nc.vector.quantize_mx(z_codes[c][:].bitcast(FP8X4), z_scales[c][:], grouped_z[c][:])

        def phase(c):
            for h in range(CHUNK // P):
                taps = slice(h * P, (h + 1) * P)
                bank = short_banks.tile([P, N], F32, name="phase_bank", tag="short")
                nc.tensor.matmul_mx(
                    bank[:], lhsT=z_codes[c][:, taps].bitcast(FP8X4), lhsT_scale=z_scales[c][:, taps],
                    rhs=w2_codes[:].bitcast(FP8X4), rhs_scale=w2_scales[:], start=True, stop=True,
                )
                turns[c, h] = ring.tile([P, N], F32, name="turns")
                whole[c, h] = ring.tile([P, N], F32, name="whole")
                nc.scalar.activation(turns[c, h][:], bank[:], ACT.Copy, scale=0.5 / math.pi, bias=0.25)
                if c < ROUNDED_ON_SCALAR:
                    nc.scalar.activation(whole[c, h][:], turns[c, h][:], ACT.Copy, scale=-1.0, bias=-ROUND)

        def round_turns(c):
            if c >= ROUNDED_ON_SCALAR:
                for h in range(CHUNK // P):
                    nc.vector.tensor_scalar(whole[c, h][:], turns[c, h][:], -1.0, -ROUND, ALU.mult, ALU.add)

        def cosine(c):
            for g in range(PAIRS):
                bank = wrap_banks.tile([P, 2, CHUNK], F32, name="wrap_bank")
                for h in range(CHUNK // P):
                    for i in range(2):
                        rows = slice((2 * g + i) * P, (2 * g + i + 1) * P)
                        terms = (magic[:], whole[c, h][:, rows], turns[c, h][:, rows])
                        for n, term in enumerate(terms):
                            nc.tensor.matmul(
                                bank[:, i, h * P : (h + 1) * P], lhsT=term, rhs=identity[:],
                                is_transpose=True, start=(n == 0), stop=(n == len(terms) - 1),
                            )
                result[c, g] = held([P, 2, CHUNK], F32, "result%d_%d" % (c, g))
                nc.scalar.activation(result[c, g][:], bank[:], ACT.Sin, scale=2.0 * math.pi)

        def finish(c):
            cols = slice(c * CHUNK, (c + 1) * CHUNK)
            banks = []
            for g in range(PAIRS):
                bank = long_banks.tile([P, 2, CHUNK], F32, name="feature_bank", tag="long")
                for i in range(2):
                    nt = 2 * g + i
                    nc.tensor.matmul_mx(
                        bank[:, i, :],
                        lhsT=w4_sb[:].bitcast(U8)[:, nt * 2 * P : (nt + 1) * 2 * P].bitcast(FP4X4),
                        lhsT_scale=w_scales[:, N + nt * P : N + (nt + 1) * P],
                        rhs=z_codes[c][:].bitcast(FP8X4), rhs_scale=z_scales[c][:], start=True, stop=True,
                    )
                banks.append(bank)
                nc.vector.tensor_tensor(
                    result[c, g][:], result[c, g][:], skip[:, 2 * g : 2 * g + 2, cols], ALU.mult
                )
            for g in range(PAIRS):
                nc.vector.tensor_tensor(result[c, g][:], result[c, g][:], banks[g][:], ALU.add)
                nc.sync.dma_start(
                    out[2 * g * P : (2 * g + 2) * P, cols].rearrange("(i p) j -> p i j", p=P), result[c, g][:]
                )

        steps = [
            (1, pick_chunk), (0, weave), (-1, phase), (-2, cosine), (0, quantise), (-1, round_turns), (-2, finish),
        ]
        for step in range(CHUNKS + 2):
            for shift, work in steps:
                if 0 <= step + shift < CHUNKS:
                    work(step + shift)
